import numpy as np
import ml_dtypes


def mxq(x, axis, fmt="e4m3"):
    dtype, down = {"e4m3": (ml_dtypes.float8_e4m3fn, 7), "e5m2": (ml_dtypes.float8_e5m2, 14)}[fmt]
    v = np.moveaxis(np.asarray(x, np.float32).astype(ml_dtypes.bfloat16).astype(np.float64), axis, -1)
    blocks = v.reshape(v.shape[:-1] + (-1, 32))
    amax = np.abs(blocks).max(-1, keepdims=True)
    byte = np.maximum(np.where(amax > 0, np.frexp(amax)[1] - 1 + 127, 0) - down, 1)
    scale = np.exp2(byte - 127.0)
    codes = (blocks / scale).astype(np.float32).astype(dtype).astype(np.float64)
    return np.moveaxis((codes * scale).reshape(v.shape), -1, axis)


WIDE = False


def mx_kscale(k):
    if not WIDE:
        return np.ones(k)
    levels = np.array([10, -10, 5, -5, 0])
    if k % 512:
        return np.exp2(np.random.permutation(np.resize(levels, k // 32))).repeat(32)
    a = np.empty((k // 512, 16))
    for p in range(k // 512):
        a[p, :8] = np.random.permutation(np.resize(levels, 8))
        for g in range(8):
            far = levels[np.abs(levels - a[p, g]) >= 10]
            a[p, g + 8] = far[np.random.randint(len(far))]
    return np.exp2(a.ravel()).repeat(32)


def f64(x):
    return np.asarray(x).astype(np.float64)


def striped8(idx):
    return np.concatenate([x.reshape(-1, 16).T for x in idx]).astype(np.uint16)


def runs(offs, k):
    lists = np.stack([offs[16 * r : 16 * r + 16].T.reshape(-1) for r in range(8)]).astype(np.int64)
    return lists[np.arange(k) % 512 // 64]


def pack_weight(w):
    k, n = w.shape
    w = f64(np.asarray(w, np.float32).astype(ml_dtypes.bfloat16)).reshape(k // 32, 32, n)
    amax = np.abs(w).max(1)
    byte = np.clip(np.where(amax > 0, np.frexp(amax)[1] - 1 + 127 - 7, 1), 1, 254)
    scaled = (w * np.exp2(127.0 - byte)[:, None, :]).reshape(k, n).astype(np.float32)
    words = np.ascontiguousarray(scaled.reshape(k // 512, 128, 4, n).transpose(0, 1, 3, 2)).astype(ml_dtypes.float8_e4m3fn).view(np.uint8)
    return words, np.ascontiguousarray(byte.astype(np.uint8).reshape(k // 512, 16, n))


def unpack_weight(words, scales):
    g, p, n, _ = words.shape
    vals = np.ascontiguousarray(words).view(ml_dtypes.float8_e4m3fn).astype(np.float64) * np.repeat(np.exp2(scales.astype(np.float64) - 127.0), 8, axis=1)[..., None]
    return vals.transpose(0, 1, 3, 2).reshape(g * 512, n)

def planes(y):
    n, m = y.shape
    v = y.astype(np.float32).astype(ml_dtypes.bfloat16).astype(np.float64).reshape(n // 32, 32, m)
    top = np.abs(v).max(1)
    byte = np.clip(np.where(top > 0, np.frexp(top)[1] - 1 + 127 - 7, 1), 1, 254)
    codes = (v * np.exp2(127.0 - byte)[:, None, :]).reshape(n, m).astype(np.float32).astype(ml_dtypes.float8_e4m3fn).view(np.uint8)
    words = codes.reshape(n // 512, 128, 4, m).transpose(0, 1, 3, 2)
    return np.ascontiguousarray(words), np.ascontiguousarray(byte.astype(np.uint8).reshape(n // 512, 16, m))


K, T, S, H, V = 512, 2048, 1024, 512, 512


def setup_inputs():
    n = np.random.standard_normal
    s = mx_kscale(K)[:, None]
    u = mx_kscale(H)
    packed_xT = pack_weight(n((K, T)) * s)
    return {
        "x_words": packed_xT[0],
        "x_scales": packed_xT[1],
        "w1": (n((K, H)) / np.sqrt(K) / s * u).astype(np.float32),
        "w2": (n((H, H)) / np.sqrt(H) / u[:, None]).astype(np.float32),
        "offs": striped8(np.stack([np.random.permutation(T)[:S] for _ in range(8)])),
    }


def reference(x_words, x_scales, w1, w2, offs):
    xq = unpack_weight(x_words, x_scales)[np.arange(K)[:, None], runs(offs, K)]
    y = mxq(f64(w1), 0, "e4m3").T @ xq
    z = np.maximum(y[:, :V], y[:, V:2 * V])
    out_0 = mxq(f64(w2), 0, "e4m3").T @ mxq(z, 0, "e4m3")
    return (out_0,) + planes(out_0)

@@ -1,0 +1,162 @@
+from contextlib import ExitStack
+
+import concourse.mybir as mybir
+
+K, T, S, H, V = 512, 2048, 1024, 512, 512
+FLOPS = 2 * K * H * S + 2 * H * H * V
+
+F32 = mybir.dt.float32
+BF16 = mybir.dt.bfloat16
+I32 = mybir.dt.int32
+U32 = mybir.dt.uint32
+U16 = mybir.dt.uint16
+U8 = mybir.dt.uint8
+FP8X4 = mybir.dt.float8_e4m3fn_x4
+MAX = mybir.AluOpType.max
+
+P = 128
+PACK = 4
+CHUNK = 128
+PIECE = 256
+HALF = 256
+
+
+def tile_picked_phpool_none_po_kernel(tc, x_words, x_scales, w1, w2, offs, out_0, out_1, out_2):
+    nc = tc.nc
+    chunks = V // CHUNK
+    with ExitStack() as ctx:
+        keep = ctx.enter_context(tc.tile_pool(name="keep", bufs=1))
+        psum_a = ctx.enter_context(tc.psum_pool(name="psum_a", bufs=3))
+        psum_b = ctx.enter_context(tc.psum_pool(name="psum_b", bufs=3))
+        psum_o = ctx.enter_context(tc.psum_pool(name="psum_o", bufs=2))
+
+        lists = keep.tile([P, S // 16], U16, name="lists")
+        nc.sync.dma_start(lists[:], offs)
+
+        scale_table = keep.tile([P, T], U8, name="scale_table", align_bytes=64)
+        nc.vector.memset(scale_table[:].bitcast(I32), 0)
+        nc.sync.dma_start(scale_table[0:P:8, :].bitcast(I32), x_scales[0].bitcast(I32))
+        x_plane = keep.tile([P, S], U8, name="x_plane", align_bytes=64)
+        nc.vector.memset(x_plane[:].bitcast(I32), 0)
+
+        def load_half(w, h, name):
+            raw = keep.tile([P, PACK, HALF], F32, name=name)
+            nc.scalar.dma_start(raw[:], w.rearrange("(p j) c -> p j c", j=PACK)[:, :, h * HALF : (h + 1) * HALF])
+            return raw
+
+        w1_raw = [load_half(w1, 0, "w1_raw0")]
+        word_table = keep.tile([P, T], I32, name="word_table", align_bytes=64)
+        nc.scalar.dma_start(word_table[:], x_words[0].rearrange("p n r -> p (n r)").bitcast(I32))
+        w1_raw.append(load_half(w1, 1, "w1_raw1"))
+        w2_raw = [load_half(w2, h, "w2_raw%d" % h) for h in range(2)]
+
+        picked_scales = keep.tile([P, S], U8, name="picked_scales", align_bytes=64)
+        nc.vector.tensor_copy(picked_scales[:], scale_table[:].indirect(lists[:]))
+        for q in range(4):
+            nc.sync.dma_start(x_plane[32 * q : 32 * q + 4, :].bitcast(I32), picked_scales[32 * q : 32 * q + 32 : 8, :].bitcast(I32))
+
+        def deal(raw, h, dealt):
+            m = HALF // PACK
+            nc.scalar.copy(
+                dealt[:].rearrange("p (t m j) -> p m j t", t=PACK, j=PACK)[:, h * m : (h + 1) * m],
+                raw[:].rearrange("p j (m t) -> p m j t", t=PACK),
+            )
+
+        x_codes = {}
+
+        def gather_words(first):
+            picked = keep.tile([P, PIECE], U32, name="x_codes%d" % first, align_bytes=64)
+            nc.vector.tensor_copy(picked[:], word_table[:].bitcast(U32).indirect(lists[:, first // 16 : (first + PIECE) // 16]))
+            x_codes[first] = picked
+
+        w1_dealt = keep.tile([P, PACK * H], BF16, name="w1_dealt", align_bytes=64)
+        w1_codes = keep.tile([P, H], U32, name="w1_codes", align_bytes=64)
+        w1_plane = keep.tile([P, H], U8, name="w1_plane", align_bytes=64)
+        w2_dealt = keep.tile([P, PACK * H], BF16, name="w2_dealt", align_bytes=64)
+        w2_codes = keep.tile([P, H], U32, name="w2_codes", align_bytes=64)
+        w2_plane = keep.tile([P, H], U8, name="w2_plane", align_bytes=64)
+        out_codes = keep.tile([P, V], U32, name="out_codes", align_bytes=64)
+        out_plane = keep.tile([P, V], U8, name="out_plane", align_bytes=64)
+
+        deal(w1_raw[0], 0, w1_dealt)
+        gather_words(0)
+        gather_words(V)
+        gather_words(PIECE)
+        deal(w1_raw[1], 1, w1_dealt)
+        for t in range(PACK):
+            cols = slice(t * P, (t + 1) * P)
+            nc.vector.quantize_mx(out=w1_codes[:, cols].bitcast(FP8X4), scales=w1_plane[:, cols], in_=w1_dealt[:, t * H : (t + 1) * H])
+        gather_words(V + PIECE)
+        deal(w2_raw[0], 0, w2_dealt)
+
+        def product(bank, codes, plane, rhs, rhs_plane):
+            for t in range(PACK):
+                cols = slice(t * P, (t + 1) * P)
+                nc.tensor.matmul_mx(out=bank[:, t, :], lhsT=codes[:, cols].bitcast(FP8X4), lhsT_scale=plane[:, cols], rhs=rhs.bitcast(FP8X4), rhs_scale=rhs_plane, start=True, stop=True)
+
+        def read(bank, first):
+            piece = first // PIECE * PIECE
+            product(bank, w1_codes, w1_plane, x_codes[piece][:, first - piece : first - piece + CHUNK], x_plane[:, first : first + CHUNK])
+
+        z, z_codes, z_plane, y, y16 = {}, {}, {}, {}, {}
+
+        def pool_reads(c):
+            bank_a = psum_a.tile([P, PACK, CHUNK], F32, name="bank_a")
+            read(bank_a, c * CHUNK)
+            bank_b = psum_b.tile([P, PACK, CHUNK], F32, name="bank_b")
+            read(bank_b, V + c * CHUNK)
+            first_read = keep.tile([P, CHUNK, PACK], F32, name="first_read%d" % c)
+            nc.scalar.copy(first_read[:], bank_a[:].rearrange("p t v -> p v t"))
+            z[c] = keep.tile([P, CHUNK, PACK], BF16, name="z%d" % c, align_bytes=64)
+            nc.vector.tensor_tensor(z[c][:], bank_b[:].rearrange("p t v -> p v t"), first_read[:], MAX)
+
+        def quantize_z(c):
+            z_codes[c] = keep.tile([P, CHUNK], U32, name="z_codes%d" % c, align_bytes=64)
+            z_plane[c] = keep.tile([P, CHUNK], U8, name="z_plane%d" % c, align_bytes=64)
+            nc.vector.quantize_mx(out=z_codes[c][:].bitcast(FP8X4), scales=z_plane[c][:], in_=z[c][:].rearrange("p v t -> p (v t)"))
+
+        def second_layer(c):
+            bank = psum_o.tile([P, PACK, CHUNK], F32, name="bank_o")
+            product(bank, w2_codes, w2_plane, z_codes[c][:], z_plane[c][:])
+            y[c] = keep.tile([P, PACK, CHUNK], F32, name="y%d" % c)
+            nc.scalar.copy(y[c][:], bank[:])
+            nc.sync.dma_start(out_0.rearrange("(p t) v -> p t v", t=PACK)[:, :, c * CHUNK : (c + 1) * CHUNK], y[c][:])
+
+        def round_y(c):
+            y16[c] = keep.tile([P, CHUNK * PACK], BF16, name="y16_%d" % c, align_bytes=64)
+            nc.vector.tensor_copy(y16[c][:].rearrange("p (g i t) -> p g t i", i=4, t=PACK), y[c][:].rearrange("p t (g i) -> p g t i", i=4))
+
+        def quantize_y(c):
+            cols = slice(c * CHUNK, (c + 1) * CHUNK)
+            nc.vector.quantize_mx(out=out_codes[:, cols].bitcast(FP8X4), scales=out_plane[:, cols], in_=y16[c][:])
+
+        def store_codes(first, last):
+            nc.sync.dma_start(out_1[0].rearrange("p n r -> p (n r)").bitcast(I32)[:, first:last], out_codes[:, first:last].bitcast(I32))
+
+        pool_reads(0)
+        deal(w2_raw[1], 1, w2_dealt)
+        pool_reads(1)
+        quantize_z(0)
+        nc.vector.quantize_mx(out=w2_codes[:].bitcast(FP8X4), scales=w2_plane[:], in_=w2_dealt[:])
+        quantize_z(1)
+        pool_reads(2)
+        second_layer(0)
+        pool_reads(3)
+        quantize_z(2)
+        second_layer(1)
+        round_y(0)
+        quantize_z(3)
+        second_layer(2)
+        round_y(1)
+        quantize_y(0)
+        second_layer(3)
+        round_y(2)
+        quantize_y(1)
+        store_codes(0, 2 * CHUNK)
+        round_y(3)
+        quantize_y(2)
+        quantize_y(3)
+        store_codes(2 * CHUNK, V)
+        for q in range(4):
+            queue = nc.sync if q % 2 else nc.scalar
+            queue.dma_start(out_2[0, 4 * q : 4 * q + 4, :].bitcast(I32), out_plane[32 * q : 32 * q + 4, :].bitcast(I32))

@@ -17,7 +17,6 @@ MAX = mybir.AluOpType.max
 P = 128
 PACK = 4
 CHUNK = 128
-PIECE = 256
 HALF = 256
 
 
@@ -26,68 +25,65 @@ def tile_picked_phpool_none_po_kernel(tc, x_words, x_scales, w1, w2, offs, out_0
     chunks = V // CHUNK
     with ExitStack() as ctx:
         keep = ctx.enter_context(tc.tile_pool(name="keep", bufs=1))
-        psum_a = ctx.enter_context(tc.psum_pool(name="psum_a", bufs=3))
-        psum_b = ctx.enter_context(tc.psum_pool(name="psum_b", bufs=3))
-        psum_o = ctx.enter_context(tc.psum_pool(name="psum_o", bufs=2))
+        psum_a = ctx.enter_context(tc.psum_pool(name="psum_a", bufs=4))
+        psum_b = ctx.enter_context(tc.psum_pool(name="psum_b", bufs=4))
 
         lists = keep.tile([P, S // 16], U16, name="lists")
         nc.sync.dma_start(lists[:], offs)
 
-        scale_table = keep.tile([P, T], U8, name="scale_table", align_bytes=64)
+        scale_table = keep.tile([P, T], U8, name="scale_table", tag="scale_table", align_bytes=64)
         nc.vector.memset(scale_table[:].bitcast(I32), 0)
-        nc.sync.dma_start(scale_table[0:P:8, :].bitcast(I32), x_scales[0].bitcast(I32))
         x_plane = keep.tile([P, S], U8, name="x_plane", align_bytes=64)
         nc.vector.memset(x_plane[:].bitcast(I32), 0)
 
-        def load_half(w, h, name):
-            raw = keep.tile([P, PACK, HALF], F32, name=name)
-            nc.scalar.dma_start(raw[:], w.rearrange("(p j) c -> p j c", j=PACK)[:, :, h * HALF : (h + 1) * HALF])
-            return raw
-
-        w1_raw = [load_half(w1, 0, "w1_raw0")]
+        w1_rows = w1.rearrange("(p j) c -> p j c", j=PACK)
+        w2_rows = w2.rearrange("(p j) c -> p j c", j=PACK)
+        w1_raw = keep.tile([P, PACK, H], F32, name="w1_raw")
+        nc.sync.dma_start(w1_raw[:, 0:1, :], w1_rows[:, 0:1, :])
+        early = keep.tile([P, 8], BF16, name="early")
+        nc.scalar.copy(early[:], w1_raw[:, 0, 0:8])
+        nc.sync.dma_start(scale_table[0:P:8, :].bitcast(I32), x_scales[0].bitcast(I32))
+        nc.sync.dma_start(w1_raw[:, 1:PACK, :], w1_rows[:, 1:PACK, :])
         word_table = keep.tile([P, T], I32, name="word_table", align_bytes=64)
-        nc.scalar.dma_start(word_table[:], x_words[0].rearrange("p n r -> p (n r)").bitcast(I32))
-        w1_raw.append(load_half(w1, 1, "w1_raw1"))
-        w2_raw = [load_half(w2, h, "w2_raw%d" % h) for h in range(2)]
+        nc.sync.dma_start(word_table[:], x_words[0].rearrange("p n r -> p (n r)").bitcast(I32))
+        w2_left = keep.tile([P, PACK, HALF], F32, name="w2_left", tag="w2_left", align_bytes=64)
+        nc.sync.dma_start(w2_left[:], w2_rows[:, :, 0:HALF])
 
         picked_scales = keep.tile([P, S], U8, name="picked_scales", align_bytes=64)
         nc.vector.tensor_copy(picked_scales[:], scale_table[:].indirect(lists[:]))
         for q in range(4):
             nc.sync.dma_start(x_plane[32 * q : 32 * q + 4, :].bitcast(I32), picked_scales[32 * q : 32 * q + 32 : 8, :].bitcast(I32))
+        w2_right = keep.tile([P, PACK, HALF], F32, name="w2_right", tag="scale_table", align_bytes=64)
+        nc.sync.dma_start(w2_right[:], w2_rows[:, :, HALF:H])
 
-        def deal(raw, h, dealt):
-            m = HALF // PACK
-            nc.scalar.copy(
-                dealt[:].rearrange("p (t m j) -> p m j t", t=PACK, j=PACK)[:, h * m : (h + 1) * m],
-                raw[:].rearrange("p j (m t) -> p m j t", t=PACK),
-            )
+        def dealt_view(dealt):
+            return dealt[:].rearrange("p (t m j) -> p m j t", t=PACK, j=PACK)
 
-        x_codes = {}
+        def raw_view(raw):
+            return raw[:].rearrange("p j (m t) -> p m j t", t=PACK)
 
-        def gather_words(first):
-            picked = keep.tile([P, PIECE], U32, name="x_codes%d" % first, align_bytes=64)
-            nc.vector.tensor_copy(picked[:], word_table[:].bitcast(U32).indirect(lists[:, first // 16 : (first + PIECE) // 16]))
-            x_codes[first] = picked
-
-        w1_dealt = keep.tile([P, PACK * H], BF16, name="w1_dealt", align_bytes=64)
+        w1_dealt = keep.tile([P, PACK * H], BF16, name="w1_dealt", tag="w1_dealt", align_bytes=64)
         w1_codes = keep.tile([P, H], U32, name="w1_codes", align_bytes=64)
         w1_plane = keep.tile([P, H], U8, name="w1_plane", align_bytes=64)
-        w2_dealt = keep.tile([P, PACK * H], BF16, name="w2_dealt", align_bytes=64)
+        w2_dealt = keep.tile([P, PACK * H], BF16, name="w2_dealt", tag="w2_dealt", align_bytes=64)
         w2_codes = keep.tile([P, H], U32, name="w2_codes", align_bytes=64)
         w2_plane = keep.tile([P, H], U8, name="w2_plane", align_bytes=64)
         out_codes = keep.tile([P, V], U32, name="out_codes", align_bytes=64)
         out_plane = keep.tile([P, V], U8, name="out_plane", align_bytes=64)
 
-        deal(w1_raw[0], 0, w1_dealt)
-        gather_words(0)
-        gather_words(V)
-        gather_words(PIECE)
-        deal(w1_raw[1], 1, w1_dealt)
-        for t in range(PACK):
-            cols = slice(t * P, (t + 1) * P)
-            nc.vector.quantize_mx(out=w1_codes[:, cols].bitcast(FP8X4), scales=w1_plane[:, cols], in_=w1_dealt[:, t * H : (t + 1) * H])
-        gather_words(V + PIECE)
-        deal(w2_raw[0], 0, w2_dealt)
+        nc.scalar.copy(dealt_view(w1_dealt)[:, :, :, 0:2], raw_view(w1_raw)[:, :, :, 0:2])
+        nc.vector.tensor_copy(dealt_view(w1_dealt)[:, :, :, 2:4], raw_view(w1_raw)[:, :, :, 2:4])
+        nc.vector.quantize_mx(out=w1_codes[:, 0:HALF].bitcast(FP8X4), scales=w1_plane[:, 0:HALF], in_=w1_dealt[:, 0 : 2 * H])
+        nc.vector.quantize_mx(out=w1_codes[:, HALF:H].bitcast(FP8X4), scales=w1_plane[:, HALF:H], in_=w1_dealt[:, 2 * H : 4 * H])
+
+        x_codes = keep.tile([P, S], U32, name="x_codes", tag="w1_dealt", align_bytes=64)
+        for first in (0, V):
+            nc.vector.tensor_copy(x_codes[:, first : first + V], word_table[:].bitcast(U32).indirect(lists[:, first // 16 : (first + V) // 16]))
+
+        m_half = HALF // PACK
+        nc.scalar.copy(dealt_view(w2_dealt)[:, 0:m_half], raw_view(w2_left))
+        nc.vector.tensor_copy(dealt_view(w2_dealt)[:, m_half : 2 * m_half], raw_view(w2_right))
+        nc.vector.quantize_mx(out=w2_codes[:].bitcast(FP8X4), scales=w2_plane[:], in_=w2_dealt[:])
 
         def product(bank, codes, plane, rhs, rhs_plane):
             for t in range(PACK):
@@ -95,36 +91,53 @@ def tile_picked_phpool_none_po_kernel(tc, x_words, x_scales, w1, w2, offs, out_0
                 nc.tensor.matmul_mx(out=bank[:, t, :], lhsT=codes[:, cols].bitcast(FP8X4), lhsT_scale=plane[:, cols], rhs=rhs.bitcast(FP8X4), rhs_scale=rhs_plane, start=True, stop=True)
 
         def read(bank, first):
-            piece = first // PIECE * PIECE
-            product(bank, w1_codes, w1_plane, x_codes[piece][:, first - piece : first - piece + CHUNK], x_plane[:, first : first + CHUNK])
+            product(bank, w1_codes, w1_plane, x_codes[:, first : first + CHUNK], x_plane[:, first : first + CHUNK])
 
-        z, z_codes, z_plane, y, y16 = {}, {}, {}, {}, {}
+        first_reads = keep.tile([P, V * PACK], F32, name="first_reads", tag="w2_left", align_bytes=64)
+        z = keep.tile([P, V * PACK], BF16, name="z", tag="w2_dealt", align_bytes=64)
+        z_codes = keep.tile([P, V], U32, name="z_codes", align_bytes=64)
+        z_plane = keep.tile([P, V], U8, name="z_plane", align_bytes=64)
+        y, y16, banks = {}, {}, {}
+
+        def values(tile, c):
+            return tile[:, c * CHUNK * PACK : (c + 1) * CHUNK * PACK]
+
+        def by_place(ap):
+            return ap.rearrange("p (v t) -> p v t", t=PACK)
+
+        def first_read(c):
+            bank = psum_a.tile([P, PACK, CHUNK], F32, name="bank_a")
+            read(bank, c * CHUNK)
+            nc.scalar.copy(by_place(values(first_reads, c)), bank[:].rearrange("p t v -> p v t"))
 
         def pool_reads(c):
-            bank_a = psum_a.tile([P, PACK, CHUNK], F32, name="bank_a")
-            read(bank_a, c * CHUNK)
-            bank_b = psum_b.tile([P, PACK, CHUNK], F32, name="bank_b")
-            read(bank_b, V + c * CHUNK)
-            first_read = keep.tile([P, CHUNK, PACK], F32, name="first_read%d" % c)
-            nc.scalar.copy(first_read[:], bank_a[:].rearrange("p t v -> p v t"))
-            z[c] = keep.tile([P, CHUNK, PACK], BF16, name="z%d" % c, align_bytes=64)
-            nc.vector.tensor_tensor(z[c][:], bank_b[:].rearrange("p t v -> p v t"), first_read[:], MAX)
+            bank = psum_b.tile([P, PACK, CHUNK], F32, name="bank_b")
+            read(bank, V + c * CHUNK)
+            nc.vector.tensor_tensor(by_place(values(z, c)), bank[:].rearrange("p t v -> p v t"), by_place(values(first_reads, c)), MAX)
 
         def quantize_z(c):
-            z_codes[c] = keep.tile([P, CHUNK], U32, name="z_codes%d" % c, align_bytes=64)
-            z_plane[c] = keep.tile([P, CHUNK], U8, name="z_plane%d" % c, align_bytes=64)
-            nc.vector.quantize_mx(out=z_codes[c][:].bitcast(FP8X4), scales=z_plane[c][:], in_=z[c][:].rearrange("p v t -> p (v t)"))
+            cols = slice(c * CHUNK, (c + 1) * CHUNK)
+            nc.vector.quantize_mx(out=z_codes[:, cols].bitcast(FP8X4), scales=z_plane[:, cols], in_=values(z, c))
+
+        def second_product(c):
+            cols = slice(c * CHUNK, (c + 1) * CHUNK)
+            bank = psum_a.tile([P, PACK, CHUNK], F32, name="bank_a")
+            product(bank, w2_codes, w2_plane, z_codes[:, cols], z_plane[:, cols])
+            return bank
 
         def second_layer(c):
-            bank = psum_o.tile([P, PACK, CHUNK], F32, name="bank_o")
-            product(bank, w2_codes, w2_plane, z_codes[c][:], z_plane[c][:])
+            banks[c] = second_product(c)
             y[c] = keep.tile([P, PACK, CHUNK], F32, name="y%d" % c)
-            nc.scalar.copy(y[c][:], bank[:])
+            nc.scalar.copy(y[c][:], banks[c][:])
             nc.sync.dma_start(out_0.rearrange("(p t) v -> p t v", t=PACK)[:, :, c * CHUNK : (c + 1) * CHUNK], y[c][:])
 
         def round_y(c):
             y16[c] = keep.tile([P, CHUNK * PACK], BF16, name="y16_%d" % c, align_bytes=64)
             nc.vector.tensor_copy(y16[c][:].rearrange("p (g i t) -> p g t i", i=4, t=PACK), y[c][:].rearrange("p t (g i) -> p g t i", i=4))
+
+        def round_bank(copy, c, bank):
+            y16[c] = keep.tile([P, CHUNK * PACK], BF16, name="y16_%d" % c, align_bytes=64)
+            copy(by_place(y16[c][:]), bank[:].rearrange("p t v -> p v t"))
 
         def quantize_y(c):
             cols = slice(c * CHUNK, (c + 1) * CHUNK)
@@ -133,29 +146,29 @@ def tile_picked_phpool_none_po_kernel(tc, x_words, x_scales, w1, w2, offs, out_0
         def store_codes(first, last):
             nc.sync.dma_start(out_1[0].rearrange("p n r -> p (n r)").bitcast(I32)[:, first:last], out_codes[:, first:last].bitcast(I32))
 
+        for c in range(chunks):
+            first_read(c)
         pool_reads(0)
-        deal(w2_raw[1], 1, w2_dealt)
         pool_reads(1)
         quantize_z(0)
-        nc.vector.quantize_mx(out=w2_codes[:].bitcast(FP8X4), scales=w2_plane[:], in_=w2_dealt[:])
-        quantize_z(1)
         pool_reads(2)
-        second_layer(0)
+        quantize_z(1)
         pool_reads(3)
         quantize_z(2)
-        second_layer(1)
-        round_y(0)
+        second_layer(0)
+        round_bank(nc.scalar.copy, 0, banks[0])
         quantize_z(3)
+        second_layer(1)
         second_layer(2)
+        second_layer(3)
         round_y(1)
         quantize_y(0)
-        second_layer(3)
-        round_y(2)
         quantize_y(1)
         store_codes(0, 2 * CHUNK)
-        round_y(3)
-        quantize_y(2)
+        round_bank(nc.vector.tensor_copy, 3, second_product(3))
+        round_y(2)
         quantize_y(3)
+        quantize_y(2)
         store_codes(2 * CHUNK, V)
         for q in range(4):
             queue = nc.sync if q % 2 else nc.scalar

@@ -18,6 +18,7 @@ P = 128
 PACK = 4
 CHUNK = 128
 HALF = 256
+LEFT = 320
 
 
 def tile_picked_phpool_none_po_kernel(tc, x_words, x_scales, w1, w2, offs, out_0, out_1, out_2):
@@ -46,15 +47,15 @@ def tile_picked_phpool_none_po_kernel(tc, x_words, x_scales, w1, w2, offs, out_0
         nc.sync.dma_start(w1_raw[:, 1:PACK, :], w1_rows[:, 1:PACK, :])
         word_table = keep.tile([P, T], I32, name="word_table", align_bytes=64)
         nc.sync.dma_start(word_table[:], x_words[0].rearrange("p n r -> p (n r)").bitcast(I32))
-        w2_left = keep.tile([P, PACK, HALF], F32, name="w2_left", tag="w2_left", align_bytes=64)
-        nc.sync.dma_start(w2_left[:], w2_rows[:, :, 0:HALF])
+        w2_left = keep.tile([P, PACK, LEFT], F32, name="w2_left", tag="w2_left", align_bytes=64)
+        nc.sync.dma_start(w2_left[:], w2_rows[:, :, 0:LEFT])
 
         picked_scales = keep.tile([P, S], U8, name="picked_scales", align_bytes=64)
         nc.vector.tensor_copy(picked_scales[:], scale_table[:].indirect(lists[:]))
         for q in range(4):
             nc.sync.dma_start(x_plane[32 * q : 32 * q + 4, :].bitcast(I32), picked_scales[32 * q : 32 * q + 32 : 8, :].bitcast(I32))
-        w2_right = keep.tile([P, PACK, HALF], F32, name="w2_right", tag="scale_table", align_bytes=64)
-        nc.sync.dma_start(w2_right[:], w2_rows[:, :, HALF:H])
+        w2_right = keep.tile([P, PACK, H - LEFT], F32, name="w2_right", tag="scale_table", align_bytes=64)
+        nc.sync.dma_start(w2_right[:], w2_rows[:, :, LEFT:H])
 
         def dealt_view(dealt):
             return dealt[:].rearrange("p (t m j) -> p m j t", t=PACK, j=PACK)
@@ -80,9 +81,9 @@ def tile_picked_phpool_none_po_kernel(tc, x_words, x_scales, w1, w2, offs, out_0
         for first in (0, V):
             nc.vector.tensor_copy(x_codes[:, first : first + V], word_table[:].bitcast(U32).indirect(lists[:, first // 16 : (first + V) // 16]))
 
-        m_half = HALF // PACK
+        m_half = LEFT // PACK
         nc.scalar.copy(dealt_view(w2_dealt)[:, 0:m_half], raw_view(w2_left))
-        nc.vector.tensor_copy(dealt_view(w2_dealt)[:, m_half : 2 * m_half], raw_view(w2_right))
+        nc.vector.tensor_copy(dealt_view(w2_dealt)[:, m_half:P], raw_view(w2_right))
         nc.vector.quantize_mx(out=w2_codes[:].bitcast(FP8X4), scales=w2_plane[:], in_=w2_dealt[:])
 
         def product(bank, codes, plane, rhs, rhs_plane):
@@ -146,10 +147,12 @@ def tile_picked_phpool_none_po_kernel(tc, x_words, x_scales, w1, w2, offs, out_0
         def store_codes(first, last):
             nc.sync.dma_start(out_1[0].rearrange("p n r -> p (n r)").bitcast(I32)[:, first:last], out_codes[:, first:last].bitcast(I32))
 
-        for c in range(chunks):
-            first_read(c)
+        first_read(0)
+        first_read(1)
         pool_reads(0)
+        first_read(2)
         pool_reads(1)
+        first_read(3)
         quantize_z(0)
         pool_reads(2)
         quantize_z(1)

@@ -18,21 +18,23 @@ P = 128
 PACK = 4
 CHUNK = 128
 HALF = 256
-LEFT = 320
+LEFT = 288
+SLOT = CHUNK * PACK * 2
+RIGHT = 5 * SLOT
+BANK = 2048
 
 
 def tile_picked_phpool_none_po_kernel(tc, x_words, x_scales, w1, w2, offs, out_0, out_1, out_2):
     nc = tc.nc
-    chunks = V // CHUNK
     with ExitStack() as ctx:
         keep = ctx.enter_context(tc.tile_pool(name="keep", bufs=1))
-        psum_a = ctx.enter_context(tc.psum_pool(name="psum_a", bufs=4))
-        psum_b = ctx.enter_context(tc.psum_pool(name="psum_b", bufs=4))
+        reuse = ctx.enter_context(tc.tile_pool(name="reuse", bufs=1))
+        psum = ctx.enter_context(tc.psum_pool(name="psum", bufs=1))
 
         lists = keep.tile([P, S // 16], U16, name="lists")
         nc.sync.dma_start(lists[:], offs)
 
-        scale_table = keep.tile([P, T], U8, name="scale_table", tag="scale_table", align_bytes=64)
+        scale_table = reuse.tile([P, T], U8, name="scale_table", offset=RIGHT, align_bytes=64)
         nc.vector.memset(scale_table[:].bitcast(I32), 0)
         x_plane = keep.tile([P, S], U8, name="x_plane", align_bytes=64)
         nc.vector.memset(x_plane[:].bitcast(I32), 0)
@@ -41,20 +43,18 @@ def tile_picked_phpool_none_po_kernel(tc, x_words, x_scales, w1, w2, offs, out_0
         w2_rows = w2.rearrange("(p j) c -> p j c", j=PACK)
         w1_raw = keep.tile([P, PACK, H], F32, name="w1_raw")
         nc.sync.dma_start(w1_raw[:, 0:1, :], w1_rows[:, 0:1, :])
-        early = keep.tile([P, 8], BF16, name="early")
-        nc.scalar.copy(early[:], w1_raw[:, 0, 0:8])
         nc.sync.dma_start(scale_table[0:P:8, :].bitcast(I32), x_scales[0].bitcast(I32))
         nc.sync.dma_start(w1_raw[:, 1:PACK, :], w1_rows[:, 1:PACK, :])
         word_table = keep.tile([P, T], I32, name="word_table", align_bytes=64)
         nc.sync.dma_start(word_table[:], x_words[0].rearrange("p n r -> p (n r)").bitcast(I32))
-        w2_left = keep.tile([P, PACK, LEFT], F32, name="w2_left", tag="w2_left", align_bytes=64)
+        w2_left = reuse.tile([P, PACK, LEFT], F32, name="w2_left", offset=0, align_bytes=64)
         nc.sync.dma_start(w2_left[:], w2_rows[:, :, 0:LEFT])
 
-        picked_scales = keep.tile([P, S], U8, name="picked_scales", align_bytes=64)
-        nc.vector.tensor_copy(picked_scales[:], scale_table[:].indirect(lists[:]))
+        picked = keep.tile([P, S], U8, name="picked", align_bytes=64)
+        nc.vector.tensor_copy(picked[:], scale_table[:].indirect(lists[:]))
         for q in range(4):
-            nc.sync.dma_start(x_plane[32 * q : 32 * q + 4, :].bitcast(I32), picked_scales[32 * q : 32 * q + 32 : 8, :].bitcast(I32))
-        w2_right = keep.tile([P, PACK, H - LEFT], F32, name="w2_right", tag="scale_table", align_bytes=64)
+            nc.sync.dma_start(x_plane[32 * q : 32 * q + 4, :].bitcast(I32), picked[32 * q : 32 * q + 32 : 8, :].bitcast(I32))
+        w2_right = reuse.tile([P, PACK, H - LEFT], F32, name="w2_right", offset=RIGHT, align_bytes=64)
         nc.sync.dma_start(w2_right[:], w2_rows[:, :, LEFT:H])
 
         def dealt_view(dealt):
@@ -66,113 +66,136 @@ def tile_picked_phpool_none_po_kernel(tc, x_words, x_scales, w1, w2, offs, out_0
         w1_dealt = keep.tile([P, PACK * H], BF16, name="w1_dealt", tag="w1_dealt", align_bytes=64)
         w1_codes = keep.tile([P, H], U32, name="w1_codes", align_bytes=64)
         w1_plane = keep.tile([P, H], U8, name="w1_plane", align_bytes=64)
-        w2_dealt = keep.tile([P, PACK * H], BF16, name="w2_dealt", tag="w2_dealt", align_bytes=64)
+        w2_dealt = keep.tile([P, PACK * H], BF16, name="w2_dealt", align_bytes=64)
         w2_codes = keep.tile([P, H], U32, name="w2_codes", align_bytes=64)
         w2_plane = keep.tile([P, H], U8, name="w2_plane", align_bytes=64)
         out_codes = keep.tile([P, V], U32, name="out_codes", align_bytes=64)
         out_plane = keep.tile([P, V], U8, name="out_plane", align_bytes=64)
 
-        nc.scalar.copy(dealt_view(w1_dealt)[:, :, :, 0:2], raw_view(w1_raw)[:, :, :, 0:2])
+        nc.scalar.copy(dealt_view(w1_dealt)[:, :, 0:1, 0:2], raw_view(w1_raw)[:, :, 0:1, 0:2])
+        nc.scalar.copy(dealt_view(w1_dealt)[:, :, 1:PACK, 0:2], raw_view(w1_raw)[:, :, 1:PACK, 0:2])
         nc.vector.tensor_copy(dealt_view(w1_dealt)[:, :, :, 2:4], raw_view(w1_raw)[:, :, :, 2:4])
         nc.vector.quantize_mx(out=w1_codes[:, 0:HALF].bitcast(FP8X4), scales=w1_plane[:, 0:HALF], in_=w1_dealt[:, 0 : 2 * H])
         nc.vector.quantize_mx(out=w1_codes[:, HALF:H].bitcast(FP8X4), scales=w1_plane[:, HALF:H], in_=w1_dealt[:, 2 * H : 4 * H])
+
 
         x_codes = keep.tile([P, S], U32, name="x_codes", tag="w1_dealt", align_bytes=64)
         for first in (0, V):
             nc.vector.tensor_copy(x_codes[:, first : first + V], word_table[:].bitcast(U32).indirect(lists[:, first // 16 : (first + V) // 16]))
 
-        m_half = LEFT // PACK
-        nc.scalar.copy(dealt_view(w2_dealt)[:, 0:m_half], raw_view(w2_left))
-        nc.vector.tensor_copy(dealt_view(w2_dealt)[:, m_half:P], raw_view(w2_right))
-        nc.vector.quantize_mx(out=w2_codes[:].bitcast(FP8X4), scales=w2_plane[:], in_=w2_dealt[:])
+        m_left = LEFT // PACK
+        nc.scalar.copy(dealt_view(w2_dealt)[:, 0:m_left], raw_view(w2_left))
+        nc.vector.tensor_copy(dealt_view(w2_dealt)[:, m_left:P], raw_view(w2_right))
 
         def product(bank, codes, plane, rhs, rhs_plane):
             for t in range(PACK):
                 cols = slice(t * P, (t + 1) * P)
                 nc.tensor.matmul_mx(out=bank[:, t, :], lhsT=codes[:, cols].bitcast(FP8X4), lhsT_scale=plane[:, cols], rhs=rhs.bitcast(FP8X4), rhs_scale=rhs_plane, start=True, stop=True)
 
-        def read(bank, first):
+        def read(c, r, b):
+            bank = psum.tile([P, PACK, CHUNK], F32, name="read%d_%d" % (r, c), offset=b * BANK)
+            first = r * V + c * CHUNK
             product(bank, w1_codes, w1_plane, x_codes[:, first : first + CHUNK], x_plane[:, first : first + CHUNK])
+            return bank
 
-        first_reads = keep.tile([P, V * PACK], F32, name="first_reads", tag="w2_left", align_bytes=64)
-        z = keep.tile([P, V * PACK], BF16, name="z", tag="w2_dealt", align_bytes=64)
         z_codes = keep.tile([P, V], U32, name="z_codes", align_bytes=64)
         z_plane = keep.tile([P, V], U8, name="z_plane", align_bytes=64)
-        y, y16, banks = {}, {}, {}
-
-        def values(tile, c):
-            return tile[:, c * CHUNK * PACK : (c + 1) * CHUNK * PACK]
+        y = keep.tile([P, PACK, V], F32, name="y")
+        y16 = keep.tile([P, V * PACK], BF16, name="y16", align_bytes=64)
+        first_reads, second_reads, z, banks = {}, {}, {}, {}
 
         def by_place(ap):
             return ap.rearrange("p (v t) -> p v t", t=PACK)
 
-        def first_read(c):
-            bank = psum_a.tile([P, PACK, CHUNK], F32, name="bank_a")
-            read(bank, c * CHUNK)
-            nc.scalar.copy(by_place(values(first_reads, c)), bank[:].rearrange("p t v -> p v t"))
+        def places_first(bank):
+            return bank[:].rearrange("p t v -> p v t")
 
-        def pool_reads(c):
-            bank = psum_b.tile([P, PACK, CHUNK], F32, name="bank_b")
-            read(bank, V + c * CHUNK)
-            nc.vector.tensor_tensor(by_place(values(z, c)), bank[:].rearrange("p t v -> p v t"), by_place(values(first_reads, c)), MAX)
+        def first_read(c, b):
+            bank = read(c, 0, b)
+            first_reads[c] = reuse.tile([P, CHUNK * PACK], BF16, name="first_reads%d" % c, offset=c * SLOT, align_bytes=64)
+            nc.scalar.copy(by_place(first_reads[c][:]), places_first(bank))
+
+        def second_read(c, b):
+            bank = read(c, 1, b)
+            second_reads[c] = keep.tile([P, CHUNK * PACK], BF16, name="second_reads%d" % c, align_bytes=64)
+            nc.scalar.copy(by_place(second_reads[c][:]), places_first(bank))
+
+        def pool_reads(c, b):
+            bank = read(c, 1, b)
+            z[c] = reuse.tile([P, CHUNK * PACK], BF16, name="z%d" % c, offset=RIGHT + c * SLOT, align_bytes=64)
+            nc.vector.tensor_tensor(by_place(z[c][:]), places_first(bank), by_place(first_reads[c][:]), MAX)
+
+        def pool_copies(c):
+            z[c] = reuse.tile([P, CHUNK * PACK], BF16, name="z%d" % c, offset=RIGHT + c * SLOT, align_bytes=64)
+            nc.vector.tensor_tensor(z[c][:], second_reads[c][:], first_reads[c][:], MAX)
 
         def quantize_z(c):
             cols = slice(c * CHUNK, (c + 1) * CHUNK)
-            nc.vector.quantize_mx(out=z_codes[:, cols].bitcast(FP8X4), scales=z_plane[:, cols], in_=values(z, c))
+            nc.vector.quantize_mx(out=z_codes[:, cols].bitcast(FP8X4), scales=z_plane[:, cols], in_=z[c][:])
 
-        def second_product(c):
-            cols = slice(c * CHUNK, (c + 1) * CHUNK)
-            bank = psum_a.tile([P, PACK, CHUNK], F32, name="bank_a")
-            product(bank, w2_codes, w2_plane, z_codes[:, cols], z_plane[:, cols])
+        def quantize_w2():
+            nc.vector.quantize_mx(out=w2_codes[:].bitcast(FP8X4), scales=w2_plane[:], in_=w2_dealt[:])
+
+        def store_y(first, last):
+            nc.sync.dma_start(out_0.rearrange("(p t) v -> p t v", t=PACK)[:, :, first:last], y[:, :, first:last])
+
+        def second_product(first, last, b):
+            bank = psum.tile([P, PACK, last - first], F32, name="result%d" % first, offset=b * BANK)
+            product(bank, w2_codes, w2_plane, z_codes[:, first:last], z_plane[:, first:last])
             return bank
 
-        def second_layer(c):
-            banks[c] = second_product(c)
-            y[c] = keep.tile([P, PACK, CHUNK], F32, name="y%d" % c)
-            nc.scalar.copy(y[c][:], banks[c][:])
-            nc.sync.dma_start(out_0.rearrange("(p t) v -> p t v", t=PACK)[:, :, c * CHUNK : (c + 1) * CHUNK], y[c][:])
+        def second_layer(c, b):
+            first, last = c * CHUNK, (c + 1) * CHUNK
+            banks[c] = second_product(first, last, b)
+            nc.scalar.copy(y[:, :, first:last], banks[c][:])
+            store_y(first, last)
 
-        def round_y(c):
-            y16[c] = keep.tile([P, CHUNK * PACK], BF16, name="y16_%d" % c, align_bytes=64)
-            nc.vector.tensor_copy(y16[c][:].rearrange("p (g i t) -> p g t i", i=4, t=PACK), y[c][:].rearrange("p t (g i) -> p g t i", i=4))
+        def round_y(first, last):
+            nc.vector.tensor_copy(y16[:, first * PACK : last * PACK].rearrange("p (g i t) -> p g t i", i=4, t=PACK), y[:, :, first:last].rearrange("p t (g i) -> p g t i", i=4))
 
-        def round_bank(copy, c, bank):
-            y16[c] = keep.tile([P, CHUNK * PACK], BF16, name="y16_%d" % c, align_bytes=64)
-            copy(by_place(y16[c][:]), bank[:].rearrange("p t v -> p v t"))
+        def round_bank(copy, bank, first, last):
+            copy(by_place(y16[:, first * PACK : last * PACK]), places_first(bank))
 
-        def quantize_y(c):
-            cols = slice(c * CHUNK, (c + 1) * CHUNK)
-            nc.vector.quantize_mx(out=out_codes[:, cols].bitcast(FP8X4), scales=out_plane[:, cols], in_=y16[c][:])
+        def last_second_layer(first, middle, last, b):
+            pair = [second_product(first, middle, b), second_product(middle, last, b + 1)]
+            nc.scalar.copy(y[:, :, first:middle], pair[0][:])
+            round_bank(nc.vector.tensor_copy, pair[1], middle, last)
+            nc.scalar.copy(y[:, :, middle:last], pair[1][:])
+            store_y(first, last)
+
+        def quantize_y(first, last):
+            nc.vector.quantize_mx(out=out_codes[:, first:last].bitcast(FP8X4), scales=out_plane[:, first:last], in_=y16[:, first * PACK : last * PACK])
 
         def store_codes(first, last):
             nc.sync.dma_start(out_1[0].rearrange("p n r -> p (n r)").bitcast(I32)[:, first:last], out_codes[:, first:last].bitcast(I32))
 
-        first_read(0)
-        first_read(1)
-        pool_reads(0)
-        first_read(2)
-        pool_reads(1)
-        first_read(3)
+        first_read(0, 0)
+        first_read(1, 1)
+        quantize_w2()
+        pool_reads(0, 4)
+        first_read(2, 2)
+        pool_reads(1, 5)
         quantize_z(0)
-        pool_reads(2)
+        second_read(2, 6)
+        first_read(3, 3)
+        pool_copies(2)
         quantize_z(1)
-        pool_reads(3)
+        pool_reads(3, 4)
         quantize_z(2)
-        second_layer(0)
-        round_bank(nc.scalar.copy, 0, banks[0])
+        second_layer(0, 6)
         quantize_z(3)
-        second_layer(1)
-        second_layer(2)
-        second_layer(3)
-        round_y(1)
-        quantize_y(0)
-        quantize_y(1)
-        store_codes(0, 2 * CHUNK)
-        round_bank(nc.vector.tensor_copy, 3, second_product(3))
-        round_y(2)
-        quantize_y(3)
-        quantize_y(2)
-        store_codes(2 * CHUNK, V)
+        second_layer(1, 0)
+        second_layer(2, 1)
+        round_y(0, 128)
+        round_y(128, 256)
+        last_second_layer(384, 448, 512, 2)
+        quantize_y(0, 256)
+        store_codes(0, 256)
+        round_y(256, 384)
+        round_y(384, 448)
+        quantize_y(256, 384)
+        quantize_y(384, 512)
+        store_codes(256, 512)
         for q in range(4):
             queue = nc.sync if q % 2 else nc.scalar
             queue.dma_start(out_2[0, 4 * q : 4 * q + 4, :].bitcast(I32), out_plane[32 * q : 32 * q + 4, :].bitcast(I32))

@@ -79,6 +79,10 @@ def tile_picked_phpool_none_po_kernel(tc, x_words, x_scales, w1, w2, offs, out_0
         nc.vector.quantize_mx(out=w1_codes[:, HALF:H].bitcast(FP8X4), scales=w1_plane[:, HALF:H], in_=w1_dealt[:, 2 * H : 4 * H])
 
 
+        warm = psum.tile([P, H], F32, name="warm", offset=7 * BANK)
+        for t in range(3):
+            nc.tensor.matmul_mx(out=warm[0:128, 0:512], lhsT=w1_codes[:, 0:128].bitcast(FP8X4), lhsT_scale=w1_plane[:, 0:128], rhs=w1_codes[:, 0:512].bitcast(FP8X4), rhs_scale=w1_plane[:, 0:512], start=True, stop=True)
+
         x_codes = keep.tile([P, S], U32, name="x_codes", tag="w1_dealt", align_bytes=64)
         for first in (0, V):
             nc.vector.tensor_copy(x_codes[:, first : first + V], word_table[:].bitcast(U32).indirect(lists[:, first // 16 : (first + V) // 16]))

@@ -18,6 +18,7 @@ P = 128
 PACK = 4
 CHUNK = 128
 HALF = 256
+SCALAR_GROUPS = 48
 LEFT = 288
 SLOT = CHUNK * PACK * 2
 RIGHT = 5 * SLOT
@@ -70,7 +71,7 @@ def tile_picked_phpool_none_po_kernel(tc, x_words, x_scales, w1, w2, offs, out_0
         w2_codes = keep.tile([P, H], U32, name="w2_codes", align_bytes=64)
         w2_plane = keep.tile([P, H], U8, name="w2_plane", align_bytes=64)
         out_codes = keep.tile([P, V], U32, name="out_codes", align_bytes=64)
-        out_plane = keep.tile([P, V], U8, name="out_plane", align_bytes=64)
+        out_planes = []
 
         nc.scalar.copy(dealt_view(w1_dealt)[:, :, 0:1, 0:2], raw_view(w1_raw)[:, :, 0:1, 0:2])
         nc.scalar.copy(dealt_view(w1_dealt)[:, :, 1:PACK, 0:2], raw_view(w1_raw)[:, :, 1:PACK, 0:2])
@@ -80,15 +81,16 @@ def tile_picked_phpool_none_po_kernel(tc, x_words, x_scales, w1, w2, offs, out_0
 
 
         warm = psum.tile([P, H], F32, name="warm", offset=7 * BANK)
-        for t in range(3):
-            nc.tensor.matmul_mx(out=warm[0:128, 0:512], lhsT=w1_codes[:, 0:128].bitcast(FP8X4), lhsT_scale=w1_plane[:, 0:128], rhs=w1_codes[:, 0:512].bitcast(FP8X4), rhs_scale=w1_plane[:, 0:512], start=True, stop=True)
+        for width in (256, 256, 512, 512):
+            nc.tensor.matmul_mx(out=warm[:, 0:width], lhsT=w1_codes[:, H - P : H].bitcast(FP8X4), lhsT_scale=w1_plane[:, H - P : H], rhs=w1_codes[:, H - width : H].bitcast(FP8X4), rhs_scale=w1_plane[:, H - width : H], start=True, stop=True)
 
         x_codes = keep.tile([P, S], U32, name="x_codes", tag="w1_dealt", align_bytes=64)
-        for first in (0, V):
-            nc.vector.tensor_copy(x_codes[:, first : first + V], word_table[:].bitcast(U32).indirect(lists[:, first // 16 : (first + V) // 16]))
+        for first, last in ((0, V), (V, V + HALF), (V + HALF, S)):
+            nc.vector.tensor_copy(x_codes[:, first:last], word_table[:].bitcast(U32).indirect(lists[:, first // 16 : last // 16]))
 
         m_left = LEFT // PACK
-        nc.scalar.copy(dealt_view(w2_dealt)[:, 0:m_left], raw_view(w2_left))
+        nc.scalar.copy(dealt_view(w2_dealt)[:, 0:SCALAR_GROUPS], raw_view(w2_left)[:, 0:SCALAR_GROUPS])
+        nc.gpsimd.tensor_copy(w2_dealt[:].rearrange("p (t m j) -> p t m j", t=PACK, j=PACK)[:, :, SCALAR_GROUPS:m_left], w2_left[:].rearrange("p j (m t) -> p t m j", t=PACK)[:, :, SCALAR_GROUPS:m_left])
         nc.vector.tensor_copy(dealt_view(w2_dealt)[:, m_left:P], raw_view(w2_right))
 
         def product(bank, codes, plane, rhs, rhs_plane):
@@ -116,7 +118,7 @@ def tile_picked_phpool_none_po_kernel(tc, x_words, x_scales, w1, w2, offs, out_0
 
         def first_read(c, b):
             bank = read(c, 0, b)
-            first_reads[c] = reuse.tile([P, CHUNK * PACK], BF16, name="first_reads%d" % c, offset=c * SLOT, align_bytes=64)
+            first_reads[c] = keep.tile([P, CHUNK * PACK], BF16, name="first_reads%d" % c, align_bytes=64)
             nc.scalar.copy(by_place(first_reads[c][:]), places_first(bank))
 
         def second_read(c, b):
@@ -168,38 +170,40 @@ def tile_picked_phpool_none_po_kernel(tc, x_words, x_scales, w1, w2, offs, out_0
             store_y(first, last)
 
         def quantize_y(first, last):
-            nc.vector.quantize_mx(out=out_codes[:, first:last].bitcast(FP8X4), scales=out_plane[:, first:last], in_=y16[:, first * PACK : last * PACK])
+            nc.vector.quantize_mx(out=out_codes[:, first:last].bitcast(FP8X4), scales=out_planes[0][:, first:last], in_=y16[:, first * PACK : last * PACK])
 
         def store_codes(first, last):
             nc.sync.dma_start(out_1[0].rearrange("p n r -> p (n r)").bitcast(I32)[:, first:last], out_codes[:, first:last].bitcast(I32))
 
         first_read(0, 0)
         first_read(1, 1)
-        quantize_w2()
         pool_reads(0, 4)
         first_read(2, 2)
-        pool_reads(1, 5)
+        quantize_w2()
         quantize_z(0)
+        pool_reads(1, 5)
         second_read(2, 6)
         first_read(3, 3)
         pool_copies(2)
         quantize_z(1)
-        pool_reads(3, 4)
+        pool_reads(3, 7)
         quantize_z(2)
-        second_layer(0, 6)
+        second_layer(0, 4)
+        round_bank(nc.scalar.copy, banks[0], 0, 128)
         quantize_z(3)
+        out_planes.append(reuse.tile([P, V], U8, name="out_plane", offset=RIGHT + 3 * SLOT, align_bytes=64))
+        quantize_y(0, 128)
+        store_codes(0, 128)
         second_layer(1, 0)
         second_layer(2, 1)
-        round_y(0, 128)
         round_y(128, 256)
         last_second_layer(384, 448, 512, 2)
-        quantize_y(0, 256)
-        store_codes(0, 256)
+        quantize_y(128, 256)
         round_y(256, 384)
         round_y(384, 448)
         quantize_y(256, 384)
         quantize_y(384, 512)
-        store_codes(256, 512)
+        store_codes(128, 512)
         for q in range(4):
             queue = nc.sync if q % 2 else nc.scalar
-            queue.dma_start(out_2[0, 4 * q : 4 * q + 4, :].bitcast(I32), out_plane[32 * q : 32 * q + 4, :].bitcast(I32))
+            queue.dma_start(out_2[0, 4 * q : 4 * q + 4, :].bitcast(I32), out_planes[0][32 * q : 32 * q + 4, :].bitcast(I32))

@@ -71,7 +71,7 @@ def tile_picked_phpool_none_po_kernel(tc, x_words, x_scales, w1, w2, offs, out_0
         w2_codes = keep.tile([P, H], U32, name="w2_codes", align_bytes=64)
         w2_plane = keep.tile([P, H], U8, name="w2_plane", align_bytes=64)
         out_codes = keep.tile([P, V], U32, name="out_codes", align_bytes=64)
-        out_planes = []
+        out_plane = keep.tile([P, V], U8, name="out_plane", align_bytes=64)
 
         nc.scalar.copy(dealt_view(w1_dealt)[:, :, 0:1, 0:2], raw_view(w1_raw)[:, :, 0:1, 0:2])
         nc.scalar.copy(dealt_view(w1_dealt)[:, :, 1:PACK, 0:2], raw_view(w1_raw)[:, :, 1:PACK, 0:2])
@@ -107,7 +107,7 @@ def tile_picked_phpool_none_po_kernel(tc, x_words, x_scales, w1, w2, offs, out_0
         z_codes = keep.tile([P, V], U32, name="z_codes", align_bytes=64)
         z_plane = keep.tile([P, V], U8, name="z_plane", align_bytes=64)
         y = keep.tile([P, PACK, V], F32, name="y")
-        y16 = keep.tile([P, V * PACK], BF16, name="y16", align_bytes=64)
+        rounded = []
         first_reads, second_reads, z, banks = {}, {}, {}, {}
 
         def by_place(ap):
@@ -157,10 +157,10 @@ def tile_picked_phpool_none_po_kernel(tc, x_words, x_scales, w1, w2, offs, out_0
             store_y(first, last)
 
         def round_y(first, last):
-            nc.vector.tensor_copy(y16[:, first * PACK : last * PACK].rearrange("p (g i t) -> p g t i", i=4, t=PACK), y[:, :, first:last].rearrange("p t (g i) -> p g t i", i=4))
+            nc.vector.tensor_copy(rounded[0][:, first * PACK : last * PACK].rearrange("p (g i t) -> p g t i", i=4, t=PACK), y[:, :, first:last].rearrange("p t (g i) -> p g t i", i=4))
 
         def round_bank(copy, bank, first, last):
-            copy(by_place(y16[:, first * PACK : last * PACK]), places_first(bank))
+            copy(by_place(rounded[0][:, first * PACK : last * PACK]), places_first(bank))
 
         def last_second_layer(first, middle, last, b):
             pair = [second_product(first, middle, b), second_product(middle, last, b + 1)]
@@ -170,7 +170,7 @@ def tile_picked_phpool_none_po_kernel(tc, x_words, x_scales, w1, w2, offs, out_0
             store_y(first, last)
 
         def quantize_y(first, last):
-            nc.vector.quantize_mx(out=out_codes[:, first:last].bitcast(FP8X4), scales=out_planes[0][:, first:last], in_=y16[:, first * PACK : last * PACK])
+            nc.vector.quantize_mx(out=out_codes[:, first:last].bitcast(FP8X4), scales=out_plane[:, first:last], in_=rounded[0][:, first * PACK : last * PACK])
 
         def store_codes(first, last):
             nc.sync.dma_start(out_1[0].rearrange("p n r -> p (n r)").bitcast(I32)[:, first:last], out_codes[:, first:last].bitcast(I32))
@@ -184,18 +184,19 @@ def tile_picked_phpool_none_po_kernel(tc, x_words, x_scales, w1, w2, offs, out_0
         pool_reads(1, 5)
         second_read(2, 6)
         first_read(3, 3)
+        second_read(3, 7)
         pool_copies(2)
         quantize_z(1)
-        pool_reads(3, 7)
+        pool_copies(3)
         quantize_z(2)
         second_layer(0, 4)
-        round_bank(nc.scalar.copy, banks[0], 0, 128)
         quantize_z(3)
-        out_planes.append(reuse.tile([P, V], U8, name="out_plane", offset=RIGHT + 3 * SLOT, align_bytes=64))
-        quantize_y(0, 128)
-        store_codes(0, 128)
         second_layer(1, 0)
         second_layer(2, 1)
+        rounded.append(reuse.tile([P, V * PACK], BF16, name="y16", offset=RIGHT + 3 * SLOT, align_bytes=64))
+        round_y(0, 128)
+        quantize_y(0, 128)
+        store_codes(0, 128)
         round_y(128, 256)
         last_second_layer(384, 448, 512, 2)
         quantize_y(128, 256)
@@ -206,4 +207,4 @@ def tile_picked_phpool_none_po_kernel(tc, x_words, x_scales, w1, w2, offs, out_0
         store_codes(128, 512)
         for q in range(4):
             queue = nc.sync if q % 2 else nc.scalar
-            queue.dma_start(out_2[0, 4 * q : 4 * q + 4, :].bitcast(I32), out_planes[0][32 * q : 32 * q + 4, :].bitcast(I32))
+            queue.dma_start(out_2[0, 4 * q : 4 * q + 4, :].bitcast(I32), out_plane[32 * q : 32 * q + 4, :].bitcast(I32))

@@ -181,10 +181,10 @@ def tile_picked_phpool_none_po_kernel(tc, x_words, x_scales, w1, w2, offs, out_0
         first_read(2, 2)
         quantize_w2()
         quantize_z(0)
-        pool_reads(1, 5)
         second_read(2, 6)
+        pool_reads(1, 5)
         first_read(3, 3)
-        second_read(3, 7)
+        second_read(3, 2)
         pool_copies(2)
         quantize_z(1)
         pool_copies(3)
@@ -196,15 +196,13 @@ def tile_picked_phpool_none_po_kernel(tc, x_words, x_scales, w1, w2, offs, out_0
         rounded.append(reuse.tile([P, V * PACK], BF16, name="y16", offset=RIGHT + 3 * SLOT, align_bytes=64))
         round_y(0, 128)
         quantize_y(0, 128)
-        store_codes(0, 128)
         round_y(128, 256)
-        last_second_layer(384, 448, 512, 2)
-        quantize_y(128, 256)
+        last_second_layer(384, 448, 512, 5)
         round_y(256, 384)
         round_y(384, 448)
-        quantize_y(256, 384)
+        quantize_y(128, 384)
         quantize_y(384, 512)
-        store_codes(128, 512)
+        store_codes(0, 512)
         for q in range(4):
             queue = nc.sync if q % 2 else nc.scalar
             queue.dma_start(out_2[0, 4 * q : 4 * q + 4, :].bitcast(I32), out_plane[32 * q : 32 * q + 4, :].bitcast(I32))

@@ -18,7 +18,7 @@ P = 128
 PACK = 4
 CHUNK = 128
 HALF = 256
-SCALAR_GROUPS = 48
+SCALAR_GROUPS = 56
 LEFT = 288
 SLOT = CHUNK * PACK * 2
 RIGHT = 5 * SLOT
@@ -204,5 +204,4 @@ def tile_picked_phpool_none_po_kernel(tc, x_words, x_scales, w1, w2, offs, out_0
         quantize_y(384, 512)
         store_codes(0, 512)
         for q in range(4):
-            queue = nc.sync if q % 2 else nc.scalar
-            queue.dma_start(out_2[0, 4 * q : 4 * q + 4, :].bitcast(I32), out_plane[32 * q : 32 * q + 4, :].bitcast(I32))
+            nc.scalar.dma_start(out_2[0, 4 * q : 4 * q + 4, :].bitcast(I32), out_plane[32 * q : 32 * q + 4, :].bitcast(I32))

@@ -23,6 +23,7 @@ LEFT = 288
 SLOT = CHUNK * PACK * 2
 RIGHT = 5 * SLOT
 BANK = 2048
+NARROW = 32
 
 
 def tile_picked_phpool_none_po_kernel(tc, x_words, x_scales, w1, w2, offs, out_0, out_1, out_2):
@@ -81,8 +82,8 @@ def tile_picked_phpool_none_po_kernel(tc, x_words, x_scales, w1, w2, offs, out_0
 
 
         warm = psum.tile([P, H], F32, name="warm", offset=7 * BANK)
-        for width in (256, 256, 512, 512):
-            nc.tensor.matmul_mx(out=warm[:, 0:width], lhsT=w1_codes[:, H - P : H].bitcast(FP8X4), lhsT_scale=w1_plane[:, H - P : H], rhs=w1_codes[:, H - width : H].bitcast(FP8X4), rhs_scale=w1_plane[:, H - width : H], start=True, stop=True)
+        for width in (128, 128, 512, 512, 512):
+            nc.tensor.matmul_mx(out=warm[0:NARROW, 0:width], lhsT=w1_codes[:, H - 64 : H - 64 + NARROW].bitcast(FP8X4), lhsT_scale=w1_plane[:, H - 64 : H - 64 + NARROW], rhs=w1_codes[:, H - width : H].bitcast(FP8X4), rhs_scale=w1_plane[:, H - width : H], start=True, stop=True)
 
         x_codes = keep.tile([P, S], U32, name="x_codes", tag="w1_dealt", align_bytes=64)
         for first, last in ((0, V), (V, V + HALF), (V + HALF, S)):

@@ -37,7 +37,7 @@ def tile_picked_phpool_none_po_kernel(tc, x_words, x_scales, w1, w2, offs, out_0
         nc.sync.dma_start(lists[:], offs)
 
         scale_table = reuse.tile([P, T], U8, name="scale_table", offset=RIGHT, align_bytes=64)
-        nc.vector.memset(scale_table[:].bitcast(I32), 0)
+        nc.gpsimd.memset(scale_table[:].bitcast(I32), 0)
         x_plane = keep.tile([P, S], U8, name="x_plane", align_bytes=64)
         nc.vector.memset(x_plane[:].bitcast(I32), 0)
 

@@ -13,12 +13,14 @@ U16 = mybir.dt.uint16
 U8 = mybir.dt.uint8
 FP8X4 = mybir.dt.float8_e4m3fn_x4
 MAX = mybir.AluOpType.max
+MULT = mybir.AluOpType.mult
+ADD = mybir.AluOpType.add
 
 P = 128
 PACK = 4
 CHUNK = 128
 HALF = 256
-SCALAR_GROUPS = 56
+SCALAR_GROUPS = 44
 LEFT = 288
 SLOT = CHUNK * PACK * 2
 RIGHT = 5 * SLOT
@@ -82,16 +84,16 @@ def tile_picked_phpool_none_po_kernel(tc, x_words, x_scales, w1, w2, offs, out_0
 
 
         warm = psum.tile([P, H], F32, name="warm", offset=7 * BANK)
-        for width in (128, 128, 512, 512, 512):
+        for width in (128, 128, 512, 512):
             nc.tensor.matmul_mx(out=warm[0:NARROW, 0:width], lhsT=w1_codes[:, H - 64 : H - 64 + NARROW].bitcast(FP8X4), lhsT_scale=w1_plane[:, H - 64 : H - 64 + NARROW], rhs=w1_codes[:, H - width : H].bitcast(FP8X4), rhs_scale=w1_plane[:, H - width : H], start=True, stop=True)
 
         x_codes = keep.tile([P, S], U32, name="x_codes", tag="w1_dealt", align_bytes=64)
-        for first, last in ((0, V), (V, V + HALF), (V + HALF, S)):
+        for first, last in ((0, HALF), (HALF, V + HALF), (V + HALF, S)):
             nc.vector.tensor_copy(x_codes[:, first:last], word_table[:].bitcast(U32).indirect(lists[:, first // 16 : last // 16]))
 
         m_left = LEFT // PACK
         nc.scalar.copy(dealt_view(w2_dealt)[:, 0:SCALAR_GROUPS], raw_view(w2_left)[:, 0:SCALAR_GROUPS])
-        nc.gpsimd.tensor_copy(w2_dealt[:].rearrange("p (t m j) -> p t m j", t=PACK, j=PACK)[:, :, SCALAR_GROUPS:m_left], w2_left[:].rearrange("p j (m t) -> p t m j", t=PACK)[:, :, SCALAR_GROUPS:m_left])
+        nc.gpsimd.tensor_scalar(w2_dealt[:].rearrange("p (t m j) -> p m t j", t=PACK, j=PACK)[:, SCALAR_GROUPS:m_left], w2_left[:].rearrange("p j (m t) -> p m t j", t=PACK)[:, SCALAR_GROUPS:m_left], 1.0, 0.0, MULT, ADD)
         nc.vector.tensor_copy(dealt_view(w2_dealt)[:, m_left:P], raw_view(w2_right))
 
         def product(bank, codes, plane, rhs, rhs_plane):
@@ -205,4 +207,4 @@ def tile_picked_phpool_none_po_kernel(tc, x_words, x_scales, w1, w2, offs, out_0
         quantize_y(384, 512)
         store_codes(0, 512)
         for q in range(4):
-            nc.scalar.dma_start(out_2[0, 4 * q : 4 * q + 4, :].bitcast(I32), out_plane[32 * q : 32 * q + 4, :].bitcast(I32))
+            (nc.sync if q == 3 else nc.scalar).dma_start(out_2[0, 4 * q : 4 * q + 4, :].bitcast(I32), out_plane[32 * q : 32 * q + 4, :].bitcast(I32))

@@ -36,7 +36,6 @@ def tile_picked_phpool_none_po_kernel(tc, x_words, x_scales, w1, w2, offs, out_0
         psum = ctx.enter_context(tc.psum_pool(name="psum", bufs=1))
 
         lists = keep.tile([P, S // 16], U16, name="lists")
-        nc.sync.dma_start(lists[:], offs)
 
         scale_table = reuse.tile([P, T], U8, name="scale_table", offset=RIGHT, align_bytes=64)
         nc.gpsimd.memset(scale_table[:].bitcast(I32), 0)
@@ -47,6 +46,7 @@ def tile_picked_phpool_none_po_kernel(tc, x_words, x_scales, w1, w2, offs, out_0
         w2_rows = w2.rearrange("(p j) c -> p j c", j=PACK)
         w1_raw = keep.tile([P, PACK, H], F32, name="w1_raw")
         nc.sync.dma_start(w1_raw[:, 0:1, :], w1_rows[:, 0:1, :])
+        nc.sync.dma_start(lists[:], offs)
         nc.sync.dma_start(scale_table[0:P:8, :].bitcast(I32), x_scales[0].bitcast(I32))
         nc.sync.dma_start(w1_raw[:, 1:PACK, :], w1_rows[:, 1:PACK, :])
         word_table = keep.tile([P, T], I32, name="word_table", align_bytes=64)

@@ -162,15 +162,12 @@ def tile_picked_phpool_none_po_kernel(tc, x_words, x_scales, w1, w2, offs, out_0
         def round_y(first, last):
             nc.vector.tensor_copy(rounded[0][:, first * PACK : last * PACK].rearrange("p (g i t) -> p g t i", i=4, t=PACK), y[:, :, first:last].rearrange("p t (g i) -> p g t i", i=4))
 
-        def round_bank(copy, bank, first, last):
-            copy(by_place(rounded[0][:, first * PACK : last * PACK]), places_first(bank))
-
         def last_second_layer(first, middle, last, b):
-            pair = [second_product(first, middle, b), second_product(middle, last, b + 1)]
-            nc.scalar.copy(y[:, :, first:middle], pair[0][:])
-            round_bank(nc.vector.tensor_copy, pair[1], middle, last)
-            nc.scalar.copy(y[:, :, middle:last], pair[1][:])
+            bank = second_product(first, last, b)
+            nc.scalar.copy(y[:, :, first:middle], bank[:, :, 0 : middle - first])
+            nc.scalar.copy(y[:, :, middle:last], bank[:, :, middle - first :])
             store_y(first, last)
+            nc.scalar.copy(by_place(rounded[0][:, middle * PACK : last * PACK]), places_first(bank)[:, middle - first :, :])
 
         def quantize_y(first, last):
             nc.vector.quantize_mx(out=out_codes[:, first:last].bitcast(FP8X4), scales=out_plane[:, first:last], in_=rounded[0][:, first * PACK : last * PACK])

@@ -157,7 +157,6 @@ def tile_picked_phpool_none_po_kernel(tc, x_words, x_scales, w1, w2, offs, out_0
             first, last = c * CHUNK, (c + 1) * CHUNK
             banks[c] = second_product(first, last, b)
             nc.scalar.copy(y[:, :, first:last], banks[c][:])
-            store_y(first, last)
 
         def round_y(first, last):
             nc.vector.tensor_copy(rounded[0][:, first * PACK : last * PACK].rearrange("p (g i t) -> p g t i", i=4, t=PACK), y[:, :, first:last].rearrange("p t (g i) -> p g t i", i=4))
@@ -166,7 +165,7 @@ def tile_picked_phpool_none_po_kernel(tc, x_words, x_scales, w1, w2, offs, out_0
             bank = second_product(first, last, b)
             nc.scalar.copy(y[:, :, first:middle], bank[:, :, 0 : middle - first])
             nc.scalar.copy(y[:, :, middle:last], bank[:, :, middle - first :])
-            store_y(first, last)
+            store_y(HALF, last)
             nc.scalar.copy(by_place(rounded[0][:, middle * PACK : last * PACK]), places_first(bank)[:, middle - first :, :])
 
         def quantize_y(first, last):
@@ -190,8 +189,10 @@ def tile_picked_phpool_none_po_kernel(tc, x_words, x_scales, w1, w2, offs, out_0
         pool_copies(3)
         quantize_z(2)
         second_layer(0, 4)
+        store_y(0, 128)
         quantize_z(3)
         second_layer(1, 0)
+        store_y(128, 256)
         second_layer(2, 1)
         rounded.append(reuse.tile([P, V * PACK], BF16, name="y16", offset=RIGHT + 3 * SLOT, align_bytes=64))
         round_y(0, 128)

@@ -203,6 +203,6 @@ def tile_picked_phpool_none_po_kernel(tc, x_words, x_scales, w1, w2, offs, out_0
         round_y(384, 448)
         quantize_y(128, 384)
         quantize_y(384, 512)
-        store_codes(0, 512)
         for q in range(4):
-            (nc.sync if q == 3 else nc.scalar).dma_start(out_2[0, 4 * q : 4 * q + 4, :].bitcast(I32), out_plane[32 * q : 32 * q + 4, :].bitcast(I32))
+            nc.sync.dma_start(out_2[0, 4 * q : 4 * q + 4, :].bitcast(I32), out_plane[32 * q : 32 * q + 4, :].bitcast(I32))
+        store_codes(0, 512)

@@ -197,6 +197,7 @@ def tile_picked_phpool_none_po_kernel(tc, x_words, x_scales, w1, w2, offs, out_0
         rounded.append(reuse.tile([P, V * PACK], BF16, name="y16", offset=RIGHT + 3 * SLOT, align_bytes=64))
         round_y(0, 128)
         quantize_y(0, 128)
+        store_codes(0, 128)
         round_y(128, 256)
         last_second_layer(384, 448, 512, 5)
         round_y(256, 384)
@@ -205,4 +206,4 @@ def tile_picked_phpool_none_po_kernel(tc, x_words, x_scales, w1, w2, offs, out_0
         quantize_y(384, 512)
         for q in range(4):
             nc.sync.dma_start(out_2[0, 4 * q : 4 * q + 4, :].bitcast(I32), out_plane[32 * q : 32 * q + 4, :].bitcast(I32))
-        store_codes(0, 512)
+        store_codes(128, 512)

@@ -20,8 +20,8 @@ P = 128
 PACK = 4
 CHUNK = 128
 HALF = 256
-SCALAR_GROUPS = 44
-LEFT = 288
+SCALAR_GROUPS = 40
+LEFT = 272
 SLOT = CHUNK * PACK * 2
 RIGHT = 5 * SLOT
 BANK = 2048
@@ -67,7 +67,7 @@ def tile_picked_phpool_none_po_kernel(tc, x_words, x_scales, w1, w2, offs, out_0
         def raw_view(raw):
             return raw[:].rearrange("p j (m t) -> p m j t", t=PACK)
 
-        w1_dealt = keep.tile([P, PACK * H], BF16, name="w1_dealt", tag="w1_dealt", align_bytes=64)
+        w1_dealt = keep.tile([P, PACK * H], BF16, name="w1_dealt", align_bytes=64)
         w1_codes = keep.tile([P, H], U32, name="w1_codes", align_bytes=64)
         w1_plane = keep.tile([P, H], U8, name="w1_plane", align_bytes=64)
         w2_dealt = keep.tile([P, PACK * H], BF16, name="w2_dealt", align_bytes=64)
@@ -87,7 +87,7 @@ def tile_picked_phpool_none_po_kernel(tc, x_words, x_scales, w1, w2, offs, out_0
         for width in (128, 128, 512, 512):
             nc.tensor.matmul_mx(out=warm[0:NARROW, 0:width], lhsT=w1_codes[:, H - 64 : H - 64 + NARROW].bitcast(FP8X4), lhsT_scale=w1_plane[:, H - 64 : H - 64 + NARROW], rhs=w1_codes[:, H - width : H].bitcast(FP8X4), rhs_scale=w1_plane[:, H - width : H], start=True, stop=True)
 
-        x_codes = keep.tile([P, S], U32, name="x_codes", tag="w1_dealt", align_bytes=64)
+        x_codes = keep.tile([P, S], U32, name="x_codes", align_bytes=64)
         for first, last in ((0, HALF), (HALF, V + HALF), (V + HALF, S)):
             nc.vector.tensor_copy(x_codes[:, first:last], word_table[:].bitcast(U32).indirect(lists[:, first // 16 : last // 16]))
 
@@ -131,19 +131,19 @@ def tile_picked_phpool_none_po_kernel(tc, x_words, x_scales, w1, w2, offs, out_0
 
         def pool_reads(c, b):
             bank = read(c, 1, b)
-            z[c] = reuse.tile([P, CHUNK * PACK], BF16, name="z%d" % c, offset=RIGHT + c * SLOT, align_bytes=64)
+            z[c] = reuse.tile([P, CHUNK * PACK], BF16, name="z%d" % c, offset=RIGHT + c * SLOT if c else RIGHT + 7 * SLOT, align_bytes=64)
             nc.vector.tensor_tensor(by_place(z[c][:]), places_first(bank), by_place(first_reads[c][:]), MAX)
 
         def pool_copies(c):
-            z[c] = reuse.tile([P, CHUNK * PACK], BF16, name="z%d" % c, offset=RIGHT + c * SLOT, align_bytes=64)
+            z[c] = reuse.tile([P, CHUNK * PACK], BF16, name="z%d" % c, offset=RIGHT + c * SLOT if c else RIGHT + 7 * SLOT, align_bytes=64)
             nc.vector.tensor_tensor(z[c][:], second_reads[c][:], first_reads[c][:], MAX)
 
         def quantize_z(c):
             cols = slice(c * CHUNK, (c + 1) * CHUNK)
             nc.vector.quantize_mx(out=z_codes[:, cols].bitcast(FP8X4), scales=z_plane[:, cols], in_=z[c][:])
 
-        def quantize_w2():
-            nc.vector.quantize_mx(out=w2_codes[:].bitcast(FP8X4), scales=w2_plane[:], in_=w2_dealt[:])
+        def quantize_w2(first):
+            nc.vector.quantize_mx(out=w2_codes[:, first : first + HALF].bitcast(FP8X4), scales=w2_plane[:, first : first + HALF], in_=w2_dealt[:, first * PACK : (first + HALF) * PACK])
 
         def store_y(first, last):
             nc.sync.dma_start(out_0.rearrange("(p t) v -> p t v", t=PACK)[:, :, first:last], y[:, :, first:last])
@@ -178,32 +178,34 @@ def tile_picked_phpool_none_po_kernel(tc, x_words, x_scales, w1, w2, offs, out_0
         first_read(1, 1)
         pool_reads(0, 4)
         first_read(2, 2)
-        quantize_w2()
+        quantize_w2(0)
         quantize_z(0)
+        quantize_w2(HALF)
         second_read(2, 6)
         pool_reads(1, 5)
         first_read(3, 3)
-        second_read(3, 2)
         pool_copies(2)
         quantize_z(1)
-        pool_copies(3)
-        quantize_z(2)
         second_layer(0, 4)
         store_y(0, 128)
+        first_rounded = keep.tile([P, CHUNK * PACK], BF16, name="first_rounded", align_bytes=64)
+        nc.scalar.copy(by_place(first_rounded[:]), places_first(banks[0]))
+        quantize_z(2)
+        pool_reads(3, 2)
+        nc.vector.quantize_mx(out=out_codes[:, 0:CHUNK].bitcast(FP8X4), scales=out_plane[:, 0:CHUNK], in_=first_rounded[:])
         quantize_z(3)
         second_layer(1, 0)
         store_y(128, 256)
         second_layer(2, 1)
-        rounded.append(reuse.tile([P, V * PACK], BF16, name="y16", offset=RIGHT + 3 * SLOT, align_bytes=64))
-        round_y(0, 128)
-        quantize_y(0, 128)
-        store_codes(0, 128)
+        rounded.append(reuse.tile([P, V * PACK], BF16, name="y16", offset=RIGHT - SLOT, align_bytes=64))
         round_y(128, 256)
+        quantize_y(128, 256)
+        store_codes(0, HALF)
         last_second_layer(384, 448, 512, 5)
         round_y(256, 384)
         round_y(384, 448)
-        quantize_y(128, 384)
+        quantize_y(256, 384)
         quantize_y(384, 512)
         for q in range(4):
             nc.sync.dma_start(out_2[0, 4 * q : 4 * q + 4, :].bitcast(I32), out_plane[32 * q : 32 * q + 4, :].bitcast(I32))
-        store_codes(128, 512)
+        store_codes(HALF, V)

from contextlib import ExitStack

import concourse.mybir as mybir

K, T, S, H, V = 512, 2048, 1024, 512, 512
FLOPS = 2 * K * H * S + 2 * H * H * V

F32 = mybir.dt.float32
BF16 = mybir.dt.bfloat16
I32 = mybir.dt.int32
U32 = mybir.dt.uint32
U16 = mybir.dt.uint16
U8 = mybir.dt.uint8
FP8X4 = mybir.dt.float8_e4m3fn_x4
MAX = mybir.AluOpType.max
MULT = mybir.AluOpType.mult
ADD = mybir.AluOpType.add

P = 128
PACK = 4
CHUNK = 128
HALF = 256
SCALAR_GROUPS = 40
LEFT = 272
SLOT = CHUNK * PACK * 2
RIGHT = 5 * SLOT
BANK = 2048
NARROW = 32


def tile_picked_phpool_none_po_kernel(tc, x_words, x_scales, w1, w2, offs, out_0, out_1, out_2):
    nc = tc.nc
    with ExitStack() as ctx:
        keep = ctx.enter_context(tc.tile_pool(name="keep", bufs=1))
        reuse = ctx.enter_context(tc.tile_pool(name="reuse", bufs=1))
        psum = ctx.enter_context(tc.psum_pool(name="psum", bufs=1))

        lists = keep.tile([P, S // 16], U16, name="lists")

        scale_table = reuse.tile([P, T], U8, name="scale_table", offset=RIGHT, align_bytes=64)
        nc.gpsimd.memset(scale_table[:].bitcast(I32), 0)
        x_plane = keep.tile([P, S], U8, name="x_plane", align_bytes=64)
        nc.vector.memset(x_plane[:].bitcast(I32), 0)

        w1_rows = w1.rearrange("(p j) c -> p j c", j=PACK)
        w2_rows = w2.rearrange("(p j) c -> p j c", j=PACK)
        w1_raw = keep.tile([P, PACK, H], F32, name="w1_raw")
        nc.sync.dma_start(w1_raw[:, 0:1, :], w1_rows[:, 0:1, :])
        nc.sync.dma_start(lists[:], offs)
        nc.sync.dma_start(scale_table[0:P:8, :].bitcast(I32), x_scales[0].bitcast(I32))
        nc.sync.dma_start(w1_raw[:, 1:PACK, :], w1_rows[:, 1:PACK, :])
        word_table = keep.tile([P, T], I32, name="word_table", align_bytes=64)
        nc.sync.dma_start(word_table[:], x_words[0].rearrange("p n r -> p (n r)").bitcast(I32))
        w2_left = reuse.tile([P, PACK, LEFT], F32, name="w2_left", offset=0, align_bytes=64)
        nc.sync.dma_start(w2_left[:], w2_rows[:, :, 0:LEFT])

        picked = keep.tile([P, S], U8, name="picked", align_bytes=64)
        nc.vector.tensor_copy(picked[:], scale_table[:].indirect(lists[:]))
        for q in range(4):
            nc.sync.dma_start(x_plane[32 * q : 32 * q + 4, :].bitcast(I32), picked[32 * q : 32 * q + 32 : 8, :].bitcast(I32))
        w2_right = reuse.tile([P, PACK, H - LEFT], F32, name="w2_right", offset=RIGHT, align_bytes=64)
        nc.sync.dma_start(w2_right[:], w2_rows[:, :, LEFT:H])

        def dealt_view(dealt):
            return dealt[:].rearrange("p (t m j) -> p m j t", t=PACK, j=PACK)

        def raw_view(raw):
            return raw[:].rearrange("p j (m t) -> p m j t", t=PACK)

        w1_dealt = keep.tile([P, PACK * H], BF16, name="w1_dealt", align_bytes=64)
        w1_codes = keep.tile([P, H], U32, name="w1_codes", align_bytes=64)
        w1_plane = keep.tile([P, H], U8, name="w1_plane", align_bytes=64)
        w2_dealt = keep.tile([P, PACK * H], BF16, name="w2_dealt", align_bytes=64)
        w2_codes = keep.tile([P, H], U32, name="w2_codes", align_bytes=64)
        w2_plane = keep.tile([P, H], U8, name="w2_plane", align_bytes=64)
        out_codes = keep.tile([P, V], U32, name="out_codes", align_bytes=64)
        out_plane = keep.tile([P, V], U8, name="out_plane", align_bytes=64)

        nc.scalar.copy(dealt_view(w1_dealt)[:, :, 0:1, 0:2], raw_view(w1_raw)[:, :, 0:1, 0:2])
        nc.scalar.copy(dealt_view(w1_dealt)[:, :, 1:PACK, 0:2], raw_view(w1_raw)[:, :, 1:PACK, 0:2])
        nc.vector.tensor_copy(dealt_view(w1_dealt)[:, :, :, 2:4], raw_view(w1_raw)[:, :, :, 2:4])
        nc.vector.quantize_mx(out=w1_codes[:, 0:HALF].bitcast(FP8X4), scales=w1_plane[:, 0:HALF], in_=w1_dealt[:, 0 : 2 * H])
        nc.vector.quantize_mx(out=w1_codes[:, HALF:H].bitcast(FP8X4), scales=w1_plane[:, HALF:H], in_=w1_dealt[:, 2 * H : 4 * H])


        warm = psum.tile([P, H], F32, name="warm", offset=7 * BANK)
        for width in (128, 128, 512, 512):
            nc.tensor.matmul_mx(out=warm[0:NARROW, 0:width], lhsT=w1_codes[:, H - 64 : H - 64 + NARROW].bitcast(FP8X4), lhsT_scale=w1_plane[:, H - 64 : H - 64 + NARROW], rhs=w1_codes[:, H - width : H].bitcast(FP8X4), rhs_scale=w1_plane[:, H - width : H], start=True, stop=True)

        x_codes = keep.tile([P, S], U32, name="x_codes", align_bytes=64)
        for first, last in ((0, HALF), (HALF, V + HALF), (V + HALF, S)):
            nc.vector.tensor_copy(x_codes[:, first:last], word_table[:].bitcast(U32).indirect(lists[:, first // 16 : last // 16]))

        m_left = LEFT // PACK
        nc.scalar.copy(dealt_view(w2_dealt)[:, 0:SCALAR_GROUPS], raw_view(w2_left)[:, 0:SCALAR_GROUPS])
        nc.gpsimd.tensor_scalar(w2_dealt[:].rearrange("p (t m j) -> p m t j", t=PACK, j=PACK)[:, SCALAR_GROUPS:m_left], w2_left[:].rearrange("p j (m t) -> p m t j", t=PACK)[:, SCALAR_GROUPS:m_left], 1.0, 0.0, MULT, ADD)
        nc.vector.tensor_copy(dealt_view(w2_dealt)[:, m_left:P], raw_view(w2_right))

        def product(bank, codes, plane, rhs, rhs_plane):
            for t in range(PACK):
                cols = slice(t * P, (t + 1) * P)
                nc.tensor.matmul_mx(out=bank[:, t, :], lhsT=codes[:, cols].bitcast(FP8X4), lhsT_scale=plane[:, cols], rhs=rhs.bitcast(FP8X4), rhs_scale=rhs_plane, start=True, stop=True)

        def read(c, r, b):
            bank = psum.tile([P, PACK, CHUNK], F32, name="read%d_%d" % (r, c), offset=b * BANK)
            first = r * V + c * CHUNK
            product(bank, w1_codes, w1_plane, x_codes[:, first : first + CHUNK], x_plane[:, first : first + CHUNK])
            return bank

        z_codes = keep.tile([P, V], U32, name="z_codes", align_bytes=64)
        z_plane = keep.tile([P, V], U8, name="z_plane", align_bytes=64)
        y = keep.tile([P, PACK, V], F32, name="y")
        rounded = []
        first_reads, second_reads, z, banks = {}, {}, {}, {}

        def by_place(ap):
            return ap.rearrange("p (v t) -> p v t", t=PACK)

        def places_first(bank):
            return bank[:].rearrange("p t v -> p v t")

        def first_read(c, b):
            bank = read(c, 0, b)
            first_reads[c] = keep.tile([P, CHUNK * PACK], BF16, name="first_reads%d" % c, align_bytes=64)
            nc.scalar.copy(by_place(first_reads[c][:]), places_first(bank))

        def second_read(c, b):
            bank = read(c, 1, b)
            second_reads[c] = keep.tile([P, CHUNK * PACK], BF16, name="second_reads%d" % c, align_bytes=64)
            nc.scalar.copy(by_place(second_reads[c][:]), places_first(bank))

        def pool_reads(c, b):
            bank = read(c, 1, b)
            z[c] = reuse.tile([P, CHUNK * PACK], BF16, name="z%d" % c, offset=RIGHT + c * SLOT if c else RIGHT + 7 * SLOT, align_bytes=64)
            nc.vector.tensor_tensor(by_place(z[c][:]), places_first(bank), by_place(first_reads[c][:]), MAX)

        def pool_copies(c):
            z[c] = reuse.tile([P, CHUNK * PACK], BF16, name="z%d" % c, offset=RIGHT + c * SLOT if c else RIGHT + 7 * SLOT, align_bytes=64)
            nc.vector.tensor_tensor(z[c][:], second_reads[c][:], first_reads[c][:], MAX)

        def quantize_z(c):
            cols = slice(c * CHUNK, (c + 1) * CHUNK)
            nc.vector.quantize_mx(out=z_codes[:, cols].bitcast(FP8X4), scales=z_plane[:, cols], in_=z[c][:])

        def quantize_w2(first):
            nc.vector.quantize_mx(out=w2_codes[:, first : first + HALF].bitcast(FP8X4), scales=w2_plane[:, first : first + HALF], in_=w2_dealt[:, first * PACK : (first + HALF) * PACK])

        def store_y(first, last):
            nc.sync.dma_start(out_0.rearrange("(p t) v -> p t v", t=PACK)[:, :, first:last], y[:, :, first:last])

        def second_product(first, last, b):
            bank = psum.tile([P, PACK, last - first], F32, name="result%d" % first, offset=b * BANK)
            product(bank, w2_codes, w2_plane, z_codes[:, first:last], z_plane[:, first:last])
            return bank

        def second_layer(c, b):
            first, last = c * CHUNK, (c + 1) * CHUNK
            banks[c] = second_product(first, last, b)
            nc.scalar.copy(y[:, :, first:last], banks[c][:])

        def round_y(first, last):
            nc.vector.tensor_copy(rounded[0][:, first * PACK : last * PACK].rearrange("p (g i t) -> p g t i", i=4, t=PACK), y[:, :, first:last].rearrange("p t (g i) -> p g t i", i=4))

        def last_second_layer(first, middle, last, b):
            bank = second_product(first, last, b)
            nc.scalar.copy(y[:, :, first:middle], bank[:, :, 0 : middle - first])
            nc.scalar.copy(y[:, :, middle:last], bank[:, :, middle - first :])
            store_y(HALF, last)
            nc.scalar.copy(by_place(rounded[0][:, middle * PACK : last * PACK]), places_first(bank)[:, middle - first :, :])

        def quantize_y(first, last):
            nc.vector.quantize_mx(out=out_codes[:, first:last].bitcast(FP8X4), scales=out_plane[:, first:last], in_=rounded[0][:, first * PACK : last * PACK])

        def store_codes(first, last):
            nc.sync.dma_start(out_1[0].rearrange("p n r -> p (n r)").bitcast(I32)[:, first:last], out_codes[:, first:last].bitcast(I32))

        first_read(0, 0)
        first_read(1, 1)
        pool_reads(0, 4)
        first_read(2, 2)
        quantize_w2(0)
        quantize_z(0)
        quantize_w2(HALF)
        second_read(2, 6)
        pool_reads(1, 5)
        first_read(3, 3)
        pool_copies(2)
        quantize_z(1)
        second_layer(0, 4)
        store_y(0, 128)
        first_rounded = keep.tile([P, CHUNK * PACK], BF16, name="first_rounded", align_bytes=64)
        nc.scalar.copy(by_place(first_rounded[:]), places_first(banks[0]))
        quantize_z(2)
        pool_reads(3, 2)
        nc.vector.quantize_mx(out=out_codes[:, 0:CHUNK].bitcast(FP8X4), scales=out_plane[:, 0:CHUNK], in_=first_rounded[:])
        quantize_z(3)
        second_layer(1, 0)
        store_y(128, 256)
        second_layer(2, 1)
        rounded.append(reuse.tile([P, V * PACK], BF16, name="y16", offset=RIGHT - SLOT, align_bytes=64))
        round_y(128, 256)
        quantize_y(128, 256)
        store_codes(0, HALF)
        last_second_layer(384, 448, 512, 5)
        round_y(256, 384)
        round_y(384, 448)
        quantize_y(256, 384)
        quantize_y(384, 512)
        for q in range(4):
            nc.sync.dma_start(out_2[0, 4 * q : 4 * q + 4, :].bitcast(I32), out_plane[32 * q : 32 * q + 4, :].bitcast(I32))
        store_codes(HALF, V)
